import numpy as np
import ml_dtypes


def mxq(x, axis, fmt="e4m3"):
    dtype, down = {"e4m3": (ml_dtypes.float8_e4m3fn, 7), "e5m2": (ml_dtypes.float8_e5m2, 14)}[fmt]
    v = np.moveaxis(np.asarray(x, np.float32).astype(ml_dtypes.bfloat16).astype(np.float64), axis, -1)
    blocks = v.reshape(v.shape[:-1] + (-1, 32))
    amax = np.abs(blocks).max(-1, keepdims=True)
    byte = np.maximum(np.where(amax > 0, np.frexp(amax)[1] - 1 + 127, 0) - down, 1)
    scale = np.exp2(byte - 127.0)
    codes = (blocks / scale).astype(np.float32).astype(dtype).astype(np.float64)
    return np.moveaxis((codes * scale).reshape(v.shape), -1, axis)


WIDE = False


def mx_kscale(k):
    if not WIDE:
        return np.ones(k)
    levels = np.array([10, -10, 5, -5, 0])
    if k % 512:
        return np.exp2(np.random.permutation(np.resize(levels, k // 32))).repeat(32)
    a = np.empty((k // 512, 16))
    for p in range(k // 512):
        a[p, :8] = np.random.permutation(np.resize(levels, 8))
        for g in range(8):
            far = levels[np.abs(levels - a[p, g]) >= 10]
            a[p, g + 8] = far[np.random.randint(len(far))]
    return np.exp2(a.ravel()).repeat(32)


def f64(x):
    return np.asarray(x).astype(np.float64)


def striped(idx):
    return np.tile(idx.reshape(-1, 16).T, (8, 1)).astype(np.uint16)


def unstriped(offs):
    return offs[:16].T.reshape(-1).astype(np.int64)


E2M1 = np.array([0.0, 0.5, 1.0, 1.5, 2.0, 3.0, 4.0, 6.0, -0.0, -0.5, -1.0, -1.5, -2.0, -3.0, -4.0, -6.0])


def pack_weight(w, fmt):
    k, n = w.shape
    w = f64(np.asarray(w, np.float32).astype(ml_dtypes.bfloat16)).reshape(k // 32, 32, n)
    amax = np.abs(w).max(1)
    if fmt == "e4m3":
        byte = np.frexp(amax)[1] - 1 + 127 - 7
    else:
        mant, ex = np.frexp(amax / 6.0)
        byte = np.where(mant > 0.5, ex, ex - 1) + 127
    byte = np.clip(np.where(amax > 0, byte, 1), 1, 254)
    scaled = (w * np.exp2(127.0 - byte)[:, None, :]).reshape(k, n).astype(np.float32)
    by_word = np.ascontiguousarray(scaled.reshape(k // 512, 128, 4, n).transpose(0, 1, 3, 2))
    if fmt == "e4m3":
        words = by_word.astype(ml_dtypes.float8_e4m3fn).view(np.uint8)
    else:
        c = by_word.astype(ml_dtypes.float4_e2m1fn).view(np.uint8) & 0xF
        words = (c[..., 0::2] | (c[..., 1::2] << 4)).reshape(k // 512, 128, 2 * n)
    return np.ascontiguousarray(words), np.ascontiguousarray(byte.astype(np.uint8).reshape(k // 512, 16, n))


def unpack_weight(words, scales, fmt):
    g, _, n = scales.shape
    words = np.ascontiguousarray(words).reshape(g, 128, n, -1)
    if fmt == "e4m3":
        vals = words.view(ml_dtypes.float8_e4m3fn).astype(np.float64)
    else:
        nib = np.empty((g, 128, n, 4), np.uint8)
        nib[..., 0::2] = words & 0xF
        nib[..., 1::2] = words >> 4
        vals = E2M1[nib]
    vals = vals * np.repeat(np.exp2(scales.astype(np.float64) - 127.0), 8, axis=1)[..., None]
    return vals.transpose(0, 1, 3, 2).reshape(g * 512, n)


def gelu(v):
    return 0.5 * v * (1.0 + np.tanh(np.sqrt(2.0 / np.pi) * (v + 0.044715 * v**3)))


def striped8(idx):
    return np.concatenate([v.reshape(-1, 16).T for v in idx]).astype(np.uint16)


def unstriped8(offs):
    return np.stack([offs[16 * g:16 * g + 16].T.reshape(-1) for g in range(8)]).astype(np.int64)


def heads(h, wgt, idx8):
    r = np.arange(h.shape[0])
    return wgt[r // 4 % 128] * h[r[:, None], idx8[r % 512 // 64]]


def put_heads(h, wgs, idx8, t2):
    r = np.arange(h.shape[0])
    page = np.zeros((h.shape[0], t2))
    page[r[:, None], idx8[r % 512 // 64]] = wgs[r // 4 % 128] * h
    return page


K, H, N, T, S, P, T2 = 1536, 512, 384, 4096, 1024, 1024, 2048

def setup_inputs():
    n = np.random.standard_normal
    s = mx_kscale(K)[:, None]
    u = mx_kscale(H)[:, None]
    d = {}
    d["tab_words"], d["tab_scales"] = pack_weight(n((K, T)) * s, "e4m3")
    d["offs"] = striped(np.random.permutation(T)[:S])
    d["w1"] = (1.5 * n((K, H)) / K**0.5 / s).astype(np.float32)
    d["w2_words"], d["w2_scales"] = pack_weight(1.5 * n((K, H)) / K**0.5 / s, "e2m1")
    d["gain"] = (1.2 * np.exp(0.3 * n(H)) * u[:, 0]).astype(np.float32)
    d["wgs"] = np.repeat(np.random.uniform(0.5, 2.0, (8, S)), 16, axis=0).astype(np.float32)
    d["offs2"] = striped8(np.stack([np.random.permutation(T2)[:S] for _ in range(8)]))
    d["wgt"] = np.repeat(np.random.uniform(0.5, 2.0, (8, P)), 16, axis=0).astype(np.float32)
    d["offs3"] = striped8(np.stack([np.random.permutation(T2)[:P] for _ in range(8)]))
    d["harvest"] = (0.8 * n((H, P)) * u).astype(np.float32)
    d["w3_words"], d["w3_scales"] = pack_weight(n((H, N)) / H**0.5 / u, "e4m3")
    d["purity"] = n((N, P)).astype(np.float32)
    d["w4"] = (n((H, N)) / H**0.5 / u).astype(np.float32)
    return d

def reference(tab_words, tab_scales, offs, w1, w2_words, w2_scales, gain, wgs, offs2, wgt, offs3, harvest, w3_words, w3_scales, purity, w4):
    v = unpack_weight(tab_words, tab_scales, "e4m3")[:, unstriped(offs)]
    a = np.tanh(mxq(f64(w1), 0, "e4m3").T @ v)
    b = np.tanh(unpack_weight(w2_words, w2_scales, "e2m1").T @ v)
    h = f64(gain)[:, None] * np.minimum(a, b)
    page = put_heads(h, f64(wgs), unstriped8(offs2), T2)
    x = heads(page, f64(wgt), unstriped8(offs3))
    z = mxq(x + f64(harvest), 0, "e4m3")
    e = unpack_weight(w3_words, w3_scales, "e4m3").T @ z
    blend = mxq(f64(w4), 0, "e4m3").T @ z
    return np.maximum(e, f64(purity)) - blend

@@ -1,0 +1,322 @@
+from contextlib import ExitStack
+
+import concourse.mybir as mybir
+from concourse.masks import make_identity
+
+K, H, N, T, S, M, T2 = 1536, 512, 384, 4096, 1024, 1024, 2048
+FLOPS = 2 * (2 * K * H * S + 2 * H * N * M)
+
+F32 = mybir.dt.float32
+BF16 = mybir.dt.bfloat16
+I32 = mybir.dt.int32
+U32 = mybir.dt.uint32
+U16 = mybir.dt.uint16
+U8 = mybir.dt.uint8
+FP8X4 = mybir.dt.float8_e4m3fn_x4
+FP4X4 = mybir.dt.float4_e2m1fn_x4
+ALU = mybir.AluOpType
+ACT = mybir.ActivationFunctionType
+
+P = 128
+PACK = 4
+PASSES = K // (P * PACK)
+BANK = 512
+CHUNK = 256
+NBLK = N // P
+
+
+def tile_list_oil_blend_sessions_kernel(
+    tc, tab_words, tab_scales, offs, w1, w2_words, w2_scales, gain, wgs, offs2, wgt, offs3,
+    harvest, w3_words, w3_scales, purity, w4, out,
+):
+    nc = tc.nc
+    with ExitStack() as ctx:
+        lists = ctx.enter_context(tc.tile_pool(name="lists", bufs=1))
+        keep = ctx.enter_context(tc.tile_pool(name="keep", bufs=1))
+        ring = ctx.enter_context(tc.tile_pool(name="ring", bufs=2))
+        psum = ctx.enter_context(tc.psum_pool(name="psum", bufs=1))
+
+        def held(name, shape, dtype, tag=None):
+            return keep.tile(shape, dtype, name=name, tag=tag or name, align_bytes=64)
+
+        def bank(name, index, shape):
+            return psum.tile(shape, F32, name=name, tag="bank%d" % index)
+
+        idx = lists.tile([P, S // 16], U16, name="idx")
+        idx2 = lists.tile([P, S // 16], U16, name="idx2")
+        idx3 = lists.tile([P, M // 16], U16, name="idx3")
+
+        tab_sc = held("tab_sc", [P, T], U8)
+        w2_sc_raw = held("w2_sc_raw", [P, PASSES, H], U8)
+        v_sc_low = [held("v_sc%d" % a, [P, S], U8) for a in range(1, PASSES)]
+        w3_sc = held("w3_sc", [P, N], U8)
+        pages = [held("page%d" % b, [P, T2], F32) for b in range(2)]
+        warm = held("warm", [P, 2], F32)
+        nc.vector.memset(tab_sc[:].bitcast(I32), 0)
+        nc.vector.memset(w2_sc_raw[:].rearrange("p a c -> p (a c)").bitcast(I32), 0)
+        nc.vector.memset(warm[:, 0:1], 0.0)
+        nc.scalar.activation(warm[:, 1:2], warm[:, 0:1], ACT.Tanh)
+        for plane in v_sc_low:
+            nc.vector.memset(plane[:].bitcast(I32), 0)
+        nc.vector.memset(w3_sc[:].bitcast(I32), 0)
+        for page in pages:
+            nc.vector.memset(page[:], 0.0)
+
+        for q in range(4):
+            nc.gpsimd.dma_start(
+                tab_sc[32 * q : 32 * q + 4 * PASSES, :].bitcast(I32),
+                tab_scales[:, 4 * q : 4 * q + 4, :].bitcast(I32),
+            )
+        for q in range(4):
+            nc.gpsimd.dma_start(
+                w2_sc_raw[32 * q : 32 * q + 4, :, :].bitcast(I32),
+                w2_scales[:, 4 * q : 4 * q + 4, :].rearrange("a r c -> r a c").bitcast(I32),
+            )
+        ident = held("ident", [P, P], F32)
+        make_identity(nc, ident[:])
+
+        tab = [held("tab%d" % a, [P, T], I32) for a in range(PASSES)]
+        w1_raw = [held("w1_raw%d" % a, [P, PACK, H], F32) for a in range(PASSES)]
+        w2_raw = held("w2_raw", [P, PASSES, 2 * H], U8)
+
+        def load_tab(a):
+            nc.sync.dma_start(tab[a][:], tab_words[a].rearrange("p t i -> p (t i)").bitcast(I32))
+
+        def load_w1(a):
+            rows = w1[a * P * PACK : (a + 1) * P * PACK, :]
+            nc.sync.dma_start(w1_raw[a][:], rows.rearrange("(p j) c -> p j c", j=PACK))
+
+        nc.sync.dma_start(idx[:], offs)
+        load_tab(0)
+        nc.sync.dma_start(w2_raw[:].bitcast(I32), w2_words.rearrange("a p c -> p a c").bitcast(I32))
+        load_w1(0)
+        load_w1(1)
+        load_tab(1)
+        load_w1(2)
+        load_tab(2)
+        wgs_sb = held("wgs_sb", [P, S], F32)
+        gain_sb = held("gain_sb", [P, PACK], F32)
+        wgt_sb = held("wgt_sb", [P, M], F32)
+        nc.sync.dma_start(gain_sb[:], gain.rearrange("(p t) -> p t", t=PACK))
+        nc.sync.dma_start(wgs_sb[:, 0:BANK], wgs[:, 0:BANK])
+        nc.sync.dma_start(idx2[:], offs2)
+        nc.sync.dma_start(wgs_sb[:, BANK:S], wgs[:, BANK:S])
+        nc.sync.dma_start(idx3[:], offs3)
+        nc.sync.dma_start(wgt_sb[:], wgt)
+        w4_raw = held("w4_raw", [P, PACK, N], F32)
+        nc.sync.dma_start(w4_raw[:], w4.rearrange("(p j) n -> p j n", j=PACK))
+        w3_q = held("w3_q", [P, N], I32)
+        nc.sync.dma_start(w3_q[:], w3_words[0].rearrange("p c i -> p (c i)").bitcast(I32))
+        for q in range(4):
+            nc.sync.dma_start(
+                w3_sc[32 * q : 32 * q + 4, :].bitcast(I32), w3_scales[0, 4 * q : 4 * q + 4, :].bitcast(I32)
+            )
+
+        v_q = {}
+        v_sc_packed = held("v_sc0", [P, S], U8)
+        v_sc = [v_sc_packed] + v_sc_low
+        w1_q = [held("w1_q%d" % a, [P, H], U32) for a in range(PASSES)]
+        w1_sc = [held("w1_sc%d" % a, [P, H], U8) for a in range(PASSES)]
+        w2_q = held("w2_q", [P, PASSES, 2 * H], U8)
+        w2_sc = held("w2_sc", [P, PASSES, H], U8)
+
+        def gather_tab(a, lo, hi):
+            if a not in v_q:
+                v_q[a] = held("v_q%d" % a, [P, S], U32, tag=("v_q0", "tab_sc", "w2_sc_raw")[a])
+            window = tab[a][:].bitcast(U32)
+            nc.vector.tensor_copy(v_q[a][:, lo:hi], window.indirect(idx[:, lo // 16 : hi // 16]))
+
+        def quantize_w1(a):
+            grouped = ring.tile([P, PACK * H], BF16, name="w1_grouped", align_bytes=64)
+            nc.scalar.copy(
+                grouped[:].rearrange("p (t m j) -> p m j t", t=PACK, j=PACK),
+                w1_raw[a][:].rearrange("p j (m t) -> p m j t", t=PACK),
+            )
+            nc.vector.quantize_mx(w1_q[a][:].bitcast(FP8X4), w1_sc[a][:], grouped[:])
+
+        gather_tab(0, 0, S)
+        nc.vector.tensor_copy(v_sc_packed[:], tab_sc[:].indirect(idx[:]))
+        live = 3 * 32 + 4
+        for a in range(1, PASSES):
+            nc.gpsimd.dma_start(
+                v_sc[a][0:live, :].bitcast(I32), v_sc_packed[4 * a : 4 * a + live, :].bitcast(I32)
+            )
+        nc.vector.tensor_copy(
+            w2_q[:].rearrange("p a (t m b) -> p a t m b", t=PACK, b=2),
+            w2_raw[:].rearrange("p a (m t b) -> p a t m b", t=PACK, b=2),
+        )
+        nc.vector.tensor_copy(
+            w2_sc[:].rearrange("p a (t m) -> p a t m", t=PACK),
+            w2_sc_raw[:].rearrange("p a (m t) -> p a t m", t=PACK),
+        )
+        quantize_w1(0)
+        quantize_w1(1)
+        gather_tab(1, 0, S)
+        quantize_w1(2)
+        gather_tab(2, 0, BANK)
+        gather_tab(2, BANK, S)
+
+        harv = held("harv", [P, PACK, M], F32, tag="tab0")
+        nc.sync.dma_start(harv[:], harvest.rearrange("(p t) m -> p t m", t=PACK))
+        res = held("res", [P, NBLK, M], F32, tag="tab1")
+        nc.sync.dma_start(res[:], purity.rearrange("(b p) m -> p b m", p=P))
+
+        def reading_pass(acc, which, t, half, a):
+            cols = slice(half * BANK, (half + 1) * BANK)
+            if which == 0:
+                lhs = w1_q[a][:, t * P : (t + 1) * P].bitcast(FP8X4)
+                lhs_sc = w1_sc[a][:, t * P : (t + 1) * P]
+            else:
+                lhs = w2_q[:, a, 2 * t * P : 2 * (t + 1) * P].bitcast(FP4X4)
+                lhs_sc = w2_sc[:, a, t * P : (t + 1) * P]
+            nc.tensor.matmul_mx(
+                acc[:], lhsT=lhs, lhsT_scale=lhs_sc, rhs=v_q[a][:, cols].bitcast(FP8X4),
+                rhs_scale=v_sc[a][:, cols], start=(a == 0), stop=(a == PASSES - 1),
+            )
+
+        readings = {}
+
+        def readings_of(pair):
+            groups = [(t, half, which) for t in (2 * pair, 2 * pair + 1) for half in range(2) for which in range(2)]
+            accs = [bank("acc%d_%d" % (pair, g), g, [P, BANK]) for g in range(8)]
+            if pair == 0:
+                order = [(a, g) for a in range(PASSES) for g in range(8)]
+            else:
+                order = [(a, g) for g in range(8) for a in range(PASSES)]
+            for a, g in order:
+                t, half, which = groups[g]
+                reading_pass(accs[g], which, t, half, a)
+            return groups, accs
+
+        scaled = {}
+
+        def scale_wgs(t, lo, hi):
+            if t not in scaled:
+                scaled[t] = held("scaled%d" % t, [P, S], F32, tag="reading%d_0" % (t - 1) if t else None)
+            nc.scalar.activation(scaled[t][:, lo:hi], wgs_sb[:, lo:hi], ACT.Copy, scale=gain_sb[:, t : t + 1])
+
+        def tanh_of(groups, accs, t):
+            for which in range(2):
+                readings[(t, which)] = held("reading%d_%d" % (t, which), [P, S], F32)
+            for g in range(8):
+                if groups[g][0] == t:
+                    half, which = groups[g][1], groups[g][2]
+                    nc.scalar.activation(readings[(t, which)][:, half * BANK : (half + 1) * BANK], accs[g][:], ACT.Tanh)
+
+        groups, accs = readings_of(0)
+        scale_wgs(0, 0, BANK)
+        tanh_of(groups, accs, 0)
+        scale_wgs(0, BANK, S)
+        tanh_of(groups, accs, 1)
+
+        weaker = {}
+        picked = {}
+
+        def weaker_of(t, lo, hi):
+            if t not in weaker:
+                weaker[t] = held("weaker%d" % t, [P, S], F32, tag="row%d" % t)
+            nc.vector.tensor_tensor(
+                weaker[t][:, lo:hi], readings[(t, 0)][:, lo:hi], readings[(t, 1)][:, lo:hi], ALU.min
+            )
+
+        def scatter(t, lo, hi):
+            nc.vector.tensor_tensor(
+                pages[t % 2][:].indirect(idx2[:, lo // 16 : hi // 16]),
+                weaker[t][:, lo:hi], scaled[t][:, lo:hi], ALU.mult,
+            )
+
+        def gather_page(t, lo, hi):
+            if t not in picked:
+                picked[t] = held("picked%d" % t, [P, M], F32, tag="row%d" % ((t + 1) % PACK))
+            nc.vector.tensor_tensor(
+                picked[t][:, lo:hi], pages[t % 2][:].indirect(idx3[:, lo // 16 : hi // 16]),
+                wgt_sb[:, lo:hi], ALU.mult,
+            )
+
+        weaker_of(0, 0, BANK)
+        scatter(0, 0, BANK)
+        weaker_of(0, BANK, S)
+        scale_wgs(1, 0, S)
+        weaker_of(1, 0, S)
+        scatter(0, BANK, S)
+        groups, accs = readings_of(1)
+        tanh_of(groups, accs, 2)
+        scale_wgs(2, 0, S)
+        weaker_of(2, 0, S)
+        scatter(1, 0, S)
+        tanh_of(groups, accs, 3)
+        scale_wgs(3, 0, S)
+        gather_page(0, 0, M)
+        weaker_of(3, 0, S)
+        scatter(2, 0, S)
+        gather_page(1, 0, M)
+
+        w4_grouped = held("w4_grouped", [P, N * PACK], BF16, tag="reading0_1")
+        nc.scalar.copy(
+            w4_grouped[:].rearrange("p (c i t) -> p c t i", i=4, t=PACK),
+            w4_raw[:].rearrange("p t (c i) -> p c t i", i=4),
+        )
+        w4_q = held("w4_q", [P, N], U32)
+        w4_sc = held("w4_sc", [P, N], U8)
+        for lo, hi in ((0, 256), (256, N)):
+            nc.vector.quantize_mx(w4_q[:, lo:hi].bitcast(FP8X4), w4_sc[:, lo:hi], w4_grouped[:, PACK * lo : PACK * hi])
+        scatter(3, 0, S)
+
+        turned = {}
+
+        def add_harvest(u, c):
+            acc = bank("sum%d_%d" % (u, c), c, [P, 2, 2, P])
+            steps = [(src, b, e) for src in range(2) for e in range(2) for b in range(2)]
+            for n, (src, b, e) in enumerate(steps):
+                cols = slice(c * CHUNK + b * P, c * CHUNK + (b + 1) * P)
+                operand = harv[:, 2 * u + e, cols] if src == 0 else picked[2 * u + e][:, cols]
+                nc.tensor.matmul(
+                    acc[:, b, e, :], lhsT=operand, rhs=ident[:], is_transpose=True,
+                    start=(n == 0), stop=(n == len(steps) - 1),
+                )
+            turned[(u, c)] = held("turned%d_%d" % (u, c), [P, 2, P, 2], BF16)
+            nc.scalar.copy(turned[(u, c)][:], acc[:].rearrange("m b e p -> m b p e"))
+
+        z = [held("z%d" % half, [P, BANK * PACK], BF16) for half in range(2)]
+
+        def turn_back(c):
+            acc = bank("back%d" % c, 4, [P, 2, 2, P])
+            for b in range(2):
+                for u in range(2):
+                    words = turned[(u, c)][:, b].rearrange("m p e -> m (p e)").bitcast(F32)
+                    nc.tensor.transpose(acc[:, b, u, :], words, ident[:])
+            words_out = z[c // 2][:].bitcast(F32)[:, (c % 2) * 2 * CHUNK : (c % 2 + 1) * 2 * CHUNK]
+            nc.scalar.copy(
+                words_out.rearrange("p (b m u) -> p b m u", b=2, u=2), acc[:].rearrange("p b u m -> p b m u")
+            )
+
+        for c in range(M // CHUNK):
+            add_harvest(0, c)
+        for c in range(M // CHUNK):
+            if c % 2 == 0:
+                gather_page(2, c * CHUNK, (c + 2) * CHUNK)
+            gather_page(3, c * CHUNK, (c + 1) * CHUNK)
+        for c in range(M // CHUNK):
+            add_harvest(1, c)
+            turn_back(c)
+
+        z_q = [held("z_q%d" % half, [P, BANK], U32) for half in range(2)]
+        z_sc = [held("z_sc%d" % half, [P, BANK], U8) for half in range(2)]
+        banks_of = ((5, 6, 7, 0, 1, 5), (2, 3, 4, 6, 7, 0))
+        for half in range(2):
+            cols = slice(half * BANK, (half + 1) * BANK)
+            nc.vector.quantize_mx(z_q[half][:].bitcast(FP8X4), z_sc[half][:], z[half][:])
+            sums = {}
+            for n, (which, b) in enumerate(((0, 0), (0, 1), (1, 0), (0, 2), (1, 1), (1, 2))):
+                sums[(which, b)] = bank("score%d_%d" % (half, n), banks_of[half][n], [P, BANK])
+                codes, plane = (w3_q, w3_sc) if which == 0 else (w4_q, w4_sc)
+                nc.tensor.matmul_mx(
+                    sums[(which, b)][:], lhsT=codes[:, b * P : (b + 1) * P].bitcast(FP8X4),
+                    lhsT_scale=plane[:, b * P : (b + 1) * P], rhs=z_q[half][:].bitcast(FP8X4),
+                    rhs_scale=z_sc[half][:], start=True, stop=True,
+                )
+                if which == 0:
+                    nc.vector.tensor_tensor(res[:, b, cols], sums[(0, b)][:], res[:, b, cols], ALU.max)
+                else:
+                    nc.vector.tensor_tensor(res[:, b, cols], res[:, b, cols], sums[(1, b)][:], ALU.subtract)
+                    nc.sync.dma_start(out[b * P : (b + 1) * P, cols], res[:, b, cols])

@@ -50,7 +50,6 @@ def tile_list_oil_blend_sessions_kernel(
         w2_sc_raw = held("w2_sc_raw", [P, PASSES, H], U8)
         v_sc_low = [held("v_sc%d" % a, [P, S], U8) for a in range(1, PASSES)]
         w3_sc = held("w3_sc", [P, N], U8)
-        pages = [held("page%d" % b, [P, T2], F32) for b in range(2)]
         warm = held("warm", [P, 2], F32)
         nc.vector.memset(tab_sc[:].bitcast(I32), 0)
         nc.vector.memset(w2_sc_raw[:].rearrange("p a c -> p (a c)").bitcast(I32), 0)
@@ -59,9 +58,9 @@ def tile_list_oil_blend_sessions_kernel(
         for plane in v_sc_low:
             nc.vector.memset(plane[:].bitcast(I32), 0)
         nc.vector.memset(w3_sc[:].bitcast(I32), 0)
-        for page in pages:
-            nc.vector.memset(page[:], 0.0)
 
+        gain_sb = held("gain_sb", [P, PACK], F32)
+        nc.gpsimd.dma_start(gain_sb[:], gain.rearrange("(p t) -> p t", t=PACK))
         for q in range(4):
             nc.gpsimd.dma_start(
                 tab_sc[32 * q : 32 * q + 4 * PASSES, :].bitcast(I32),
@@ -72,45 +71,33 @@ def tile_list_oil_blend_sessions_kernel(
                 w2_sc_raw[32 * q : 32 * q + 4, :, :].bitcast(I32),
                 w2_scales[:, 4 * q : 4 * q + 4, :].rearrange("a r c -> r a c").bitcast(I32),
             )
-        ident = held("ident", [P, P], F32)
-        make_identity(nc, ident[:])
 
         tab = [held("tab%d" % a, [P, T], I32) for a in range(PASSES)]
         w1_raw = [held("w1_raw%d" % a, [P, PACK, H], F32) for a in range(PASSES)]
         w2_raw = held("w2_raw", [P, PASSES, 2 * H], U8)
-
-        def load_tab(a):
-            nc.sync.dma_start(tab[a][:], tab_words[a].rearrange("p t i -> p (t i)").bitcast(I32))
-
-        def load_w1(a):
-            rows = w1[a * P * PACK : (a + 1) * P * PACK, :]
-            nc.sync.dma_start(w1_raw[a][:], rows.rearrange("(p j) c -> p j c", j=PACK))
+        wgs_sb = held("wgs_sb", [P, S], F32)
+        wgt_sb = held("wgt_sb", [P, M], F32)
+        w4_raw = held("w4_raw", [P, PACK, N], F32)
+        w3_q = held("w3_q", [P, N], I32)
+        harv = held("harv", [P, PACK, M], F32)
+        res = held("res", [P, NBLK, M], F32)
 
         nc.sync.dma_start(idx[:], offs)
-        load_tab(0)
-        nc.sync.dma_start(w2_raw[:].bitcast(I32), w2_words.rearrange("a p c -> p a c").bitcast(I32))
-        load_w1(0)
-        load_w1(1)
-        load_tab(1)
-        load_w1(2)
-        load_tab(2)
-        wgs_sb = held("wgs_sb", [P, S], F32)
-        gain_sb = held("gain_sb", [P, PACK], F32)
-        wgt_sb = held("wgt_sb", [P, M], F32)
-        nc.sync.dma_start(gain_sb[:], gain.rearrange("(p t) -> p t", t=PACK))
+        for a in range(PASSES):
+            nc.sync.dma_start(tab[a][:], tab_words[a].rearrange("p t i -> p (t i)").bitcast(I32))
+            if a == 0:
+                nc.sync.dma_start(w2_raw[:].bitcast(I32), w2_words.rearrange("a p c -> p a c").bitcast(I32))
+            rows = w1[a * P * PACK : (a + 1) * P * PACK, :]
+            nc.sync.dma_start(w1_raw[a][:], rows.rearrange("(p j) c -> p j c", j=PACK))
         nc.sync.dma_start(wgs_sb[:, 0:BANK], wgs[:, 0:BANK])
         nc.sync.dma_start(idx2[:], offs2)
         nc.sync.dma_start(wgs_sb[:, BANK:S], wgs[:, BANK:S])
         nc.sync.dma_start(idx3[:], offs3)
         nc.sync.dma_start(wgt_sb[:], wgt)
-        w4_raw = held("w4_raw", [P, PACK, N], F32)
+        nc.sync.dma_start(harv[:], harvest.rearrange("(p t) m -> p t m", t=PACK))
         nc.sync.dma_start(w4_raw[:], w4.rearrange("(p j) n -> p j n", j=PACK))
-        w3_q = held("w3_q", [P, N], I32)
         nc.sync.dma_start(w3_q[:], w3_words[0].rearrange("p c i -> p (c i)").bitcast(I32))
-        for q in range(4):
-            nc.sync.dma_start(
-                w3_sc[32 * q : 32 * q + 4, :].bitcast(I32), w3_scales[0, 4 * q : 4 * q + 4, :].bitcast(I32)
-            )
+        nc.sync.dma_start(res[:], purity.rearrange("(b p) m -> p b m", p=P))
 
         v_q = {}
         v_sc_packed = held("v_sc0", [P, S], U8)
@@ -136,30 +123,47 @@ def tile_list_oil_blend_sessions_kernel(
 
         gather_tab(0, 0, S)
         nc.vector.tensor_copy(v_sc_packed[:], tab_sc[:].indirect(idx[:]))
-        live = 3 * 32 + 4
+        live = 112
         for a in range(1, PASSES):
             nc.gpsimd.dma_start(
                 v_sc[a][0:live, :].bitcast(I32), v_sc_packed[4 * a : 4 * a + live, :].bitcast(I32)
             )
+        for q in range(4):
+            nc.gpsimd.dma_start(
+                w3_sc[32 * q : 32 * q + 4, :].bitcast(I32), w3_scales[0, 4 * q : 4 * q + 4, :].bitcast(I32)
+            )
+        ident = held("ident", [P, P], F32)
+        make_identity(nc, ident[:])
         nc.vector.tensor_copy(
-            w2_q[:].rearrange("p a (t m b) -> p a t m b", t=PACK, b=2),
-            w2_raw[:].rearrange("p a (m t b) -> p a t m b", t=PACK, b=2),
+            w2_q[:].bitcast(U16).rearrange("p a (t m) -> p a t m", t=PACK),
+            w2_raw[:].bitcast(U16).rearrange("p a (m t) -> p a t m", t=PACK),
         )
         nc.vector.tensor_copy(
             w2_sc[:].rearrange("p a (t m) -> p a t m", t=PACK),
             w2_sc_raw[:].rearrange("p a (m t) -> p a t m", t=PACK),
         )
+        pages = [held("page%d" % b, [P, T2], F32, tag=("tab0", "w2_raw")[b]) for b in range(2)]
+        for page in pages:
+            nc.vector.memset(page[:], 0.0)
         quantize_w1(0)
-        quantize_w1(1)
         gather_tab(1, 0, S)
-        quantize_w1(2)
+        quantize_w1(1)
         gather_tab(2, 0, BANK)
         gather_tab(2, BANK, S)
-
-        harv = held("harv", [P, PACK, M], F32, tag="tab0")
-        nc.sync.dma_start(harv[:], harvest.rearrange("(p t) m -> p t m", t=PACK))
-        res = held("res", [P, NBLK, M], F32, tag="tab1")
-        nc.sync.dma_start(res[:], purity.rearrange("(b p) m -> p b m", p=P))
+        last = PASSES - 1
+        first_grouped = held("first_grouped", [P, PACK * P], BF16)
+        by_slot = w1_raw[last][:].rearrange("p j (m t) -> p m j t", t=PACK)
+        nc.vector.tensor_copy(first_grouped[:].rearrange("p (m j) -> p m j", j=PACK), by_slot[:, :, :, 0])
+        nc.vector.quantize_mx(w1_q[last][:, 0:P].bitcast(FP8X4), w1_sc[last][:, 0:P], first_grouped[:])
+        rest_grouped = held("rest_grouped", [P, (PACK - 1) * PACK * P], BF16, tag="first_grouped")
+        nc.vector.tensor_copy(
+            rest_grouped[:].rearrange("p (t m j) -> p m j t", t=PACK - 1, j=PACK), by_slot[:, :, :, 1:PACK]
+        )
+        for lo, hi in ((1, 2), (2, PACK)):
+            nc.vector.quantize_mx(
+                w1_q[last][:, lo * P : hi * P].bitcast(FP8X4), w1_sc[last][:, lo * P : hi * P],
+                rest_grouped[:, (lo - 1) * PACK * P : (hi - 1) * PACK * P],
+            )
 
         def reading_pass(acc, which, t, half, a):
             cols = slice(half * BANK, (half + 1) * BANK)
@@ -176,38 +180,33 @@ def tile_list_oil_blend_sessions_kernel(
 
         readings = {}
 
-        def readings_of(pair):
-            groups = [(t, half, which) for t in (2 * pair, 2 * pair + 1) for half in range(2) for which in range(2)]
-            accs = [bank("acc%d_%d" % (pair, g), g, [P, BANK]) for g in range(8)]
-            if pair == 0:
-                order = [(a, g) for a in range(PASSES) for g in range(8)]
-            else:
-                order = [(a, g) for g in range(8) for a in range(PASSES)]
-            for a, g in order:
-                t, half, which = groups[g]
-                reading_pass(accs[g], which, t, half, a)
-            return groups, accs
+        def readings_of(t):
+            groups = [(which, half) for which in (1, 0) for half in range(2)]
+            accs = [bank("acc%d_%d" % (t, g), g, [P, BANK]) for g in range(len(groups))]
+            for a in range(PASSES):
+                for g, (which, half) in enumerate(groups):
+                    reading_pass(accs[g], which, t, half, a)
+            for which in range(2):
+                readings[(t, which)] = held(
+                    "reading%d_%d" % (t, which), [P, S], F32, tag="w1_raw%d" % which if t == PACK - 1 else None
+                )
+            for g, (which, half) in enumerate(groups):
+                nc.scalar.activation(readings[(t, which)][:, half * BANK : (half + 1) * BANK], accs[g][:], ACT.Tanh)
 
         scaled = {}
 
         def scale_wgs(t, lo, hi):
             if t not in scaled:
                 scaled[t] = held("scaled%d" % t, [P, S], F32, tag="reading%d_0" % (t - 1) if t else None)
-            nc.scalar.activation(scaled[t][:, lo:hi], wgs_sb[:, lo:hi], ACT.Copy, scale=gain_sb[:, t : t + 1])
+            if t == 0:
+                nc.vector.tensor_scalar_mul(scaled[t][:, lo:hi], wgs_sb[:, lo:hi], gain_sb[:, t : t + 1])
+            else:
+                nc.scalar.activation(scaled[t][:, lo:hi], wgs_sb[:, lo:hi], ACT.Copy, scale=gain_sb[:, t : t + 1])
 
-        def tanh_of(groups, accs, t):
-            for which in range(2):
-                readings[(t, which)] = held("reading%d_%d" % (t, which), [P, S], F32)
-            for g in range(8):
-                if groups[g][0] == t:
-                    half, which = groups[g][1], groups[g][2]
-                    nc.scalar.activation(readings[(t, which)][:, half * BANK : (half + 1) * BANK], accs[g][:], ACT.Tanh)
-
-        groups, accs = readings_of(0)
         scale_wgs(0, 0, BANK)
-        tanh_of(groups, accs, 0)
+        readings_of(0)
         scale_wgs(0, BANK, S)
-        tanh_of(groups, accs, 1)
+        readings_of(1)
 
         weaker = {}
         picked = {}
@@ -239,12 +238,11 @@ def tile_list_oil_blend_sessions_kernel(
         scale_wgs(1, 0, S)
         weaker_of(1, 0, S)
         scatter(0, BANK, S)
-        groups, accs = readings_of(1)
-        tanh_of(groups, accs, 2)
+        readings_of(2)
         scale_wgs(2, 0, S)
         weaker_of(2, 0, S)
         scatter(1, 0, S)
-        tanh_of(groups, accs, 3)
+        readings_of(3)
         scale_wgs(3, 0, S)
         gather_page(0, 0, M)
         weaker_of(3, 0, S)
@@ -277,32 +275,38 @@ def tile_list_oil_blend_sessions_kernel(
             turned[(u, c)] = held("turned%d_%d" % (u, c), [P, 2, P, 2], BF16)
             nc.scalar.copy(turned[(u, c)][:], acc[:].rearrange("m b e p -> m b p e"))
 
-        z = [held("z%d" % half, [P, BANK * PACK], BF16) for half in range(2)]
+        z = [held("z%d" % half, [P, BANK * PACK], BF16, tag="w1_raw%d" % half) for half in range(2)]
 
-        def turn_back(c):
-            acc = bank("back%d" % c, 4, [P, 2, 2, P])
+        backs = {}
+
+        def turn_back(u, c):
+            if u == 0:
+                backs[c] = bank("back%d" % c, 4 + c, [P, 2, 2, P])
             for b in range(2):
-                for u in range(2):
-                    words = turned[(u, c)][:, b].rearrange("m p e -> m (p e)").bitcast(F32)
-                    nc.tensor.transpose(acc[:, b, u, :], words, ident[:])
+                words = turned[(u, c)][:, b].rearrange("m p e -> m (p e)").bitcast(F32)
+                nc.tensor.transpose(backs[c][:, b, u, :], words, ident[:])
+
+        def weave(c):
             words_out = z[c // 2][:].bitcast(F32)[:, (c % 2) * 2 * CHUNK : (c % 2 + 1) * 2 * CHUNK]
             nc.scalar.copy(
-                words_out.rearrange("p (b m u) -> p b m u", b=2, u=2), acc[:].rearrange("p b u m -> p b m u")
+                words_out.rearrange("p (b m u) -> p b m u", b=2, u=2), backs[c][:].rearrange("p b u m -> p b m u")
             )
 
         for c in range(M // CHUNK):
             add_harvest(0, c)
+            turn_back(0, c)
         for c in range(M // CHUNK):
             if c % 2 == 0:
                 gather_page(2, c * CHUNK, (c + 2) * CHUNK)
             gather_page(3, c * CHUNK, (c + 1) * CHUNK)
         for c in range(M // CHUNK):
             add_harvest(1, c)
-            turn_back(c)
+            turn_back(1, c)
+            weave(c)
 
         z_q = [held("z_q%d" % half, [P, BANK], U32) for half in range(2)]
         z_sc = [held("z_sc%d" % half, [P, BANK], U8) for half in range(2)]
-        banks_of = ((5, 6, 7, 0, 1, 5), (2, 3, 4, 6, 7, 0))
+        banks_of = ((0, 1, 4, 5, 0, 1), (2, 3, 6, 7, 4, 5))
         for half in range(2):
             cols = slice(half * BANK, (half + 1) * BANK)
             nc.vector.quantize_mx(z_q[half][:].bitcast(FP8X4), z_sc[half][:], z[half][:])

from contextlib import ExitStack

import concourse.mybir as mybir
from concourse.masks import make_identity

K, H, N, T, S, M, T2 = 1536, 512, 384, 4096, 1024, 1024, 2048
FLOPS = 2 * (2 * K * H * S + 2 * H * N * M)

F32 = mybir.dt.float32
BF16 = mybir.dt.bfloat16
I32 = mybir.dt.int32
U32 = mybir.dt.uint32
U16 = mybir.dt.uint16
U8 = mybir.dt.uint8
FP8X4 = mybir.dt.float8_e4m3fn_x4
FP4X4 = mybir.dt.float4_e2m1fn_x4
ALU = mybir.AluOpType
ACT = mybir.ActivationFunctionType

P = 128
PACK = 4
PASSES = K // (P * PACK)
BANK = 512
CHUNK = 256
NBLK = N // P


def tile_list_oil_blend_sessions_kernel(
    tc, tab_words, tab_scales, offs, w1, w2_words, w2_scales, gain, wgs, offs2, wgt, offs3,
    harvest, w3_words, w3_scales, purity, w4, out,
):
    nc = tc.nc
    with ExitStack() as ctx:
        lists = ctx.enter_context(tc.tile_pool(name="lists", bufs=1))
        keep = ctx.enter_context(tc.tile_pool(name="keep", bufs=1))
        ring = ctx.enter_context(tc.tile_pool(name="ring", bufs=2))
        psum = ctx.enter_context(tc.psum_pool(name="psum", bufs=1))

        def held(name, shape, dtype, tag=None):
            return keep.tile(shape, dtype, name=name, tag=tag or name, align_bytes=64)

        def bank(name, index, shape):
            return psum.tile(shape, F32, name=name, tag="bank%d" % index)

        idx = lists.tile([P, S // 16], U16, name="idx")
        idx2 = lists.tile([P, S // 16], U16, name="idx2")
        idx3 = lists.tile([P, M // 16], U16, name="idx3")

        tab_sc = held("tab_sc", [P, T], U8)
        w2_sc_raw = held("w2_sc_raw", [P, PASSES, H], U8)
        v_sc_low = [held("v_sc%d" % a, [P, S], U8) for a in range(1, PASSES)]
        w3_sc = held("w3_sc", [P, N], U8)
        warm = held("warm", [P, 2], F32)
        nc.vector.memset(tab_sc[:].bitcast(I32), 0)
        nc.vector.memset(w2_sc_raw[:].rearrange("p a c -> p (a c)").bitcast(I32), 0)
        nc.vector.memset(warm[:, 0:1], 0.0)
        nc.scalar.activation(warm[:, 1:2], warm[:, 0:1], ACT.Tanh)
        for plane in v_sc_low:
            nc.vector.memset(plane[:].bitcast(I32), 0)
        nc.vector.memset(w3_sc[:].bitcast(I32), 0)

        gain_sb = held("gain_sb", [P, PACK], F32)
        nc.gpsimd.dma_start(gain_sb[:], gain.rearrange("(p t) -> p t", t=PACK))
        for q in range(4):
            nc.gpsimd.dma_start(
                tab_sc[32 * q : 32 * q + 4 * PASSES, :].bitcast(I32),
                tab_scales[:, 4 * q : 4 * q + 4, :].bitcast(I32),
            )
        for q in range(4):
            nc.gpsimd.dma_start(
                w2_sc_raw[32 * q : 32 * q + 4, :, :].bitcast(I32),
                w2_scales[:, 4 * q : 4 * q + 4, :].rearrange("a r c -> r a c").bitcast(I32),
            )

        tab = [held("tab%d" % a, [P, T], I32) for a in range(PASSES)]
        w1_raw = [held("w1_raw%d" % a, [P, PACK, H], F32) for a in range(PASSES)]
        w2_raw = held("w2_raw", [P, PASSES, 2 * H], U8)
        wgs_sb = held("wgs_sb", [P, S], F32)
        wgt_sb = held("wgt_sb", [P, M], F32)
        w4_raw = held("w4_raw", [P, PACK, N], F32)
        w3_q = held("w3_q", [P, N], I32)
        harv = held("harv", [P, PACK, M], F32)
        res = held("res", [P, NBLK, M], F32)

        nc.sync.dma_start(idx[:], offs)
        for a in range(PASSES):
            nc.sync.dma_start(tab[a][:], tab_words[a].rearrange("p t i -> p (t i)").bitcast(I32))
            if a == 0:
                nc.sync.dma_start(w2_raw[:].bitcast(I32), w2_words.rearrange("a p c -> p a c").bitcast(I32))
            rows = w1[a * P * PACK : (a + 1) * P * PACK, :]
            nc.sync.dma_start(w1_raw[a][:], rows.rearrange("(p j) c -> p j c", j=PACK))
        nc.sync.dma_start(wgs_sb[:, 0:BANK], wgs[:, 0:BANK])
        nc.sync.dma_start(idx2[:], offs2)
        nc.sync.dma_start(wgs_sb[:, BANK:S], wgs[:, BANK:S])
        nc.sync.dma_start(idx3[:], offs3)
        nc.sync.dma_start(wgt_sb[:], wgt)
        nc.sync.dma_start(harv[:], harvest.rearrange("(p t) m -> p t m", t=PACK))
        nc.sync.dma_start(w4_raw[:], w4.rearrange("(p j) n -> p j n", j=PACK))
        nc.sync.dma_start(w3_q[:], w3_words[0].rearrange("p c i -> p (c i)").bitcast(I32))
        nc.sync.dma_start(res[:], purity.rearrange("(b p) m -> p b m", p=P))

        v_q = {}
        v_sc_packed = held("v_sc0", [P, S], U8)
        v_sc = [v_sc_packed] + v_sc_low
        w1_q = [held("w1_q%d" % a, [P, H], U32) for a in range(PASSES)]
        w1_sc = [held("w1_sc%d" % a, [P, H], U8) for a in range(PASSES)]
        w2_q = held("w2_q", [P, PASSES, 2 * H], U8)
        w2_sc = held("w2_sc", [P, PASSES, H], U8)

        def gather_tab(a, lo, hi):
            if a not in v_q:
                v_q[a] = held("v_q%d" % a, [P, S], U32, tag=("v_q0", "tab_sc", "w2_sc_raw")[a])
            window = tab[a][:].bitcast(U32)
            nc.vector.tensor_copy(v_q[a][:, lo:hi], window.indirect(idx[:, lo // 16 : hi // 16]))

        def quantize_w1(a):
            grouped = ring.tile([P, PACK * H], BF16, name="w1_grouped", align_bytes=64)
            nc.scalar.copy(
                grouped[:].rearrange("p (t m j) -> p m j t", t=PACK, j=PACK),
                w1_raw[a][:].rearrange("p j (m t) -> p m j t", t=PACK),
            )
            nc.vector.quantize_mx(w1_q[a][:].bitcast(FP8X4), w1_sc[a][:], grouped[:])

        gather_tab(0, 0, S)
        nc.vector.tensor_copy(v_sc_packed[:], tab_sc[:].indirect(idx[:]))
        live = 112
        for a in range(1, PASSES):
            nc.gpsimd.dma_start(
                v_sc[a][0:live, :].bitcast(I32), v_sc_packed[4 * a : 4 * a + live, :].bitcast(I32)
            )
        for q in range(4):
            nc.gpsimd.dma_start(
                w3_sc[32 * q : 32 * q + 4, :].bitcast(I32), w3_scales[0, 4 * q : 4 * q + 4, :].bitcast(I32)
            )
        ident = held("ident", [P, P], F32)
        make_identity(nc, ident[:])
        nc.vector.tensor_copy(
            w2_q[:].bitcast(U16).rearrange("p a (t m) -> p a t m", t=PACK),
            w2_raw[:].bitcast(U16).rearrange("p a (m t) -> p a t m", t=PACK),
        )
        nc.vector.tensor_copy(
            w2_sc[:].rearrange("p a (t m) -> p a t m", t=PACK),
            w2_sc_raw[:].rearrange("p a (m t) -> p a t m", t=PACK),
        )
        pages = [held("page%d" % b, [P, T2], F32, tag=("tab0", "w2_raw")[b]) for b in range(2)]
        for page in pages:
            nc.vector.memset(page[:], 0.0)
        quantize_w1(0)
        gather_tab(1, 0, S)
        quantize_w1(1)
        gather_tab(2, 0, BANK)
        gather_tab(2, BANK, S)
        last = PASSES - 1
        first_grouped = held("first_grouped", [P, PACK * P], BF16)
        by_slot = w1_raw[last][:].rearrange("p j (m t) -> p m j t", t=PACK)
        nc.vector.tensor_copy(first_grouped[:].rearrange("p (m j) -> p m j", j=PACK), by_slot[:, :, :, 0])
        nc.vector.quantize_mx(w1_q[last][:, 0:P].bitcast(FP8X4), w1_sc[last][:, 0:P], first_grouped[:])
        rest_grouped = held("rest_grouped", [P, (PACK - 1) * PACK * P], BF16, tag="first_grouped")
        nc.vector.tensor_copy(
            rest_grouped[:].rearrange("p (t m j) -> p m j t", t=PACK - 1, j=PACK), by_slot[:, :, :, 1:PACK]
        )
        for lo, hi in ((1, 2), (2, PACK)):
            nc.vector.quantize_mx(
                w1_q[last][:, lo * P : hi * P].bitcast(FP8X4), w1_sc[last][:, lo * P : hi * P],
                rest_grouped[:, (lo - 1) * PACK * P : (hi - 1) * PACK * P],
            )

        def reading_pass(acc, which, t, half, a):
            cols = slice(half * BANK, (half + 1) * BANK)
            if which == 0:
                lhs = w1_q[a][:, t * P : (t + 1) * P].bitcast(FP8X4)
                lhs_sc = w1_sc[a][:, t * P : (t + 1) * P]
            else:
                lhs = w2_q[:, a, 2 * t * P : 2 * (t + 1) * P].bitcast(FP4X4)
                lhs_sc = w2_sc[:, a, t * P : (t + 1) * P]
            nc.tensor.matmul_mx(
                acc[:], lhsT=lhs, lhsT_scale=lhs_sc, rhs=v_q[a][:, cols].bitcast(FP8X4),
                rhs_scale=v_sc[a][:, cols], start=(a == 0), stop=(a == PASSES - 1),
            )

        readings = {}

        def readings_of(t):
            groups = [(which, half) for which in (1, 0) for half in range(2)]
            accs = [bank("acc%d_%d" % (t, g), g, [P, BANK]) for g in range(len(groups))]
            for a in range(PASSES):
                for g, (which, half) in enumerate(groups):
                    reading_pass(accs[g], which, t, half, a)
            for which in range(2):
                readings[(t, which)] = held(
                    "reading%d_%d" % (t, which), [P, S], F32, tag="w1_raw%d" % which if t == PACK - 1 else None
                )
            for g, (which, half) in enumerate(groups):
                nc.scalar.activation(readings[(t, which)][:, half * BANK : (half + 1) * BANK], accs[g][:], ACT.Tanh)

        scaled = {}

        def scale_wgs(t, lo, hi):
            if t not in scaled:
                scaled[t] = held("scaled%d" % t, [P, S], F32, tag="reading%d_0" % (t - 1) if t else None)
            if t == 0:
                nc.vector.tensor_scalar_mul(scaled[t][:, lo:hi], wgs_sb[:, lo:hi], gain_sb[:, t : t + 1])
            else:
                nc.scalar.activation(scaled[t][:, lo:hi], wgs_sb[:, lo:hi], ACT.Copy, scale=gain_sb[:, t : t + 1])

        scale_wgs(0, 0, BANK)
        readings_of(0)
        scale_wgs(0, BANK, S)
        readings_of(1)

        weaker = {}
        picked = {}

        def weaker_of(t, lo, hi):
            if t not in weaker:
                weaker[t] = held("weaker%d" % t, [P, S], F32, tag="row%d" % t)
            nc.vector.tensor_tensor(
                weaker[t][:, lo:hi], readings[(t, 0)][:, lo:hi], readings[(t, 1)][:, lo:hi], ALU.min
            )

        def scatter(t, lo, hi):
            nc.vector.tensor_tensor(
                pages[t % 2][:].indirect(idx2[:, lo // 16 : hi // 16]),
                weaker[t][:, lo:hi], scaled[t][:, lo:hi], ALU.mult,
            )

        def gather_page(t, lo, hi):
            if t not in picked:
                picked[t] = held("picked%d" % t, [P, M], F32, tag="row%d" % ((t + 1) % PACK))
            nc.vector.tensor_tensor(
                picked[t][:, lo:hi], pages[t % 2][:].indirect(idx3[:, lo // 16 : hi // 16]),
                wgt_sb[:, lo:hi], ALU.mult,
            )

        weaker_of(0, 0, BANK)
        scatter(0, 0, BANK)
        weaker_of(0, BANK, S)
        scale_wgs(1, 0, S)
        weaker_of(1, 0, S)
        scatter(0, BANK, S)
        readings_of(2)
        scale_wgs(2, 0, S)
        weaker_of(2, 0, S)
        scatter(1, 0, S)
        readings_of(3)
        scale_wgs(3, 0, S)
        gather_page(0, 0, M)
        weaker_of(3, 0, S)
        scatter(2, 0, S)
        gather_page(1, 0, M)

        w4_grouped = held("w4_grouped", [P, N * PACK], BF16, tag="reading0_1")
        nc.scalar.copy(
            w4_grouped[:].rearrange("p (c i t) -> p c t i", i=4, t=PACK),
            w4_raw[:].rearrange("p t (c i) -> p c t i", i=4),
        )
        w4_q = held("w4_q", [P, N], U32)
        w4_sc = held("w4_sc", [P, N], U8)
        for lo, hi in ((0, 256), (256, N)):
            nc.vector.quantize_mx(w4_q[:, lo:hi].bitcast(FP8X4), w4_sc[:, lo:hi], w4_grouped[:, PACK * lo : PACK * hi])
        scatter(3, 0, S)

        turned = {}

        def add_harvest(u, c):
            acc = bank("sum%d_%d" % (u, c), c, [P, 2, 2, P])
            steps = [(src, b, e) for src in range(2) for e in range(2) for b in range(2)]
            for n, (src, b, e) in enumerate(steps):
                cols = slice(c * CHUNK + b * P, c * CHUNK + (b + 1) * P)
                operand = harv[:, 2 * u + e, cols] if src == 0 else picked[2 * u + e][:, cols]
                nc.tensor.matmul(
                    acc[:, b, e, :], lhsT=operand, rhs=ident[:], is_transpose=True,
                    start=(n == 0), stop=(n == len(steps) - 1),
                )
            turned[(u, c)] = held("turned%d_%d" % (u, c), [P, 2, P, 2], BF16)
            nc.scalar.copy(turned[(u, c)][:], acc[:].rearrange("m b e p -> m b p e"))

        z = [held("z%d" % half, [P, BANK * PACK], BF16, tag="w1_raw%d" % half) for half in range(2)]

        backs = {}

        def turn_back(u, c):
            if u == 0:
                backs[c] = bank("back%d" % c, 4 + c, [P, 2, 2, P])
            for b in range(2):
                words = turned[(u, c)][:, b].rearrange("m p e -> m (p e)").bitcast(F32)
                nc.tensor.transpose(backs[c][:, b, u, :], words, ident[:])

        def weave(c):
            words_out = z[c // 2][:].bitcast(F32)[:, (c % 2) * 2 * CHUNK : (c % 2 + 1) * 2 * CHUNK]
            nc.scalar.copy(
                words_out.rearrange("p (b m u) -> p b m u", b=2, u=2), backs[c][:].rearrange("p b u m -> p b m u")
            )

        for c in range(M // CHUNK):
            add_harvest(0, c)
            turn_back(0, c)
        for c in range(M // CHUNK):
            if c % 2 == 0:
                gather_page(2, c * CHUNK, (c + 2) * CHUNK)
            gather_page(3, c * CHUNK, (c + 1) * CHUNK)
        for c in range(M // CHUNK):
            add_harvest(1, c)
            turn_back(1, c)
            weave(c)

        z_q = [held("z_q%d" % half, [P, BANK], U32) for half in range(2)]
        z_sc = [held("z_sc%d" % half, [P, BANK], U8) for half in range(2)]
        banks_of = ((0, 1, 4, 5, 0, 1), (2, 3, 6, 7, 4, 5))
        for half in range(2):
            cols = slice(half * BANK, (half + 1) * BANK)
            nc.vector.quantize_mx(z_q[half][:].bitcast(FP8X4), z_sc[half][:], z[half][:])
            sums = {}
            for n, (which, b) in enumerate(((0, 0), (0, 1), (1, 0), (0, 2), (1, 1), (1, 2))):
                sums[(which, b)] = bank("score%d_%d" % (half, n), banks_of[half][n], [P, BANK])
                codes, plane = (w3_q, w3_sc) if which == 0 else (w4_q, w4_sc)
                nc.tensor.matmul_mx(
                    sums[(which, b)][:], lhsT=codes[:, b * P : (b + 1) * P].bitcast(FP8X4),
                    lhsT_scale=plane[:, b * P : (b + 1) * P], rhs=z_q[half][:].bitcast(FP8X4),
                    rhs_scale=z_sc[half][:], start=True, stop=True,
                )
                if which == 0:
                    nc.vector.tensor_tensor(res[:, b, cols], sums[(0, b)][:], res[:, b, cols], ALU.max)
                else:
                    nc.vector.tensor_tensor(res[:, b, cols], res[:, b, cols], sums[(1, b)][:], ALU.subtract)
                    nc.sync.dma_start(out[b * P : (b + 1) * P, cols], res[:, b, cols])
